import numpy as np
import ml_dtypes


def mxq(x, axis, fmt="e4m3"):
    dtype, down = {"e4m3": (ml_dtypes.float8_e4m3fn, 7), "e5m2": (ml_dtypes.float8_e5m2, 14)}[fmt]
    v = np.moveaxis(np.asarray(x, np.float32).astype(ml_dtypes.bfloat16).astype(np.float64), axis, -1)
    blocks = v.reshape(v.shape[:-1] + (-1, 32))
    amax = np.abs(blocks).max(-1, keepdims=True)
    byte = np.maximum(np.where(amax > 0, np.frexp(amax)[1] - 1 + 127, 0) - down, 1)
    scale = np.exp2(byte - 127.0)
    codes = (blocks / scale).astype(np.float32).astype(dtype).astype(np.float64)
    return np.moveaxis((codes * scale).reshape(v.shape), -1, axis)


WIDE = False


def mx_kscale(k):
    if not WIDE:
        return np.ones(k)
    levels = np.array([10, -10, 5, -5, 0])
    if k % 512:
        return np.exp2(np.random.permutation(np.resize(levels, k // 32))).repeat(32)
    a = np.empty((k // 512, 16))
    for p in range(k // 512):
        a[p, :8] = np.random.permutation(np.resize(levels, 8))
        for g in range(8):
            far = levels[np.abs(levels - a[p, g]) >= 10]
            a[p, g + 8] = far[np.random.randint(len(far))]
    return np.exp2(a.ravel()).repeat(32)


BF16 = ml_dtypes.bfloat16


def bf(x):
    return np.asarray(x, np.float32).astype(BF16)


def f64(x):
    return np.asarray(x).astype(np.float64)


E2M1 = np.array([0.0, 0.5, 1.0, 1.5, 2.0, 3.0, 4.0, 6.0, -0.0, -0.5, -1.0, -1.5, -2.0, -3.0, -4.0, -6.0])


def pack_weight(w, fmt):
    k, n = w.shape
    w = f64(bf(w)).reshape(k // 32, 32, n)
    amax = np.abs(w).max(1)
    if fmt == "e4m3":
        byte = np.frexp(amax)[1] - 1 + 127 - 7
    else:
        mant, ex = np.frexp(amax / 6.0)
        byte = np.where(mant > 0.5, ex, ex - 1) + 127
    byte = np.clip(np.where(amax > 0, byte, 1), 1, 254)
    scaled = (w * np.exp2(127.0 - byte)[:, None, :]).reshape(k, n).astype(np.float32)
    by_word = np.ascontiguousarray(scaled.reshape(k // 512, 128, 4, n).transpose(0, 1, 3, 2))
    if fmt == "e4m3":
        words = by_word.astype(ml_dtypes.float8_e4m3fn).view(np.uint8)
    else:
        c = by_word.astype(ml_dtypes.float4_e2m1fn).view(np.uint8) & 0xF
        words = c[..., 0::2] | (c[..., 1::2] << 4)
    return np.ascontiguousarray(words), np.ascontiguousarray(byte.astype(np.uint8).reshape(k // 512, 16, n))


def unpack_weight(words, scales, fmt):
    g, p, n, _ = words.shape
    if fmt == "e4m3":
        vals = np.ascontiguousarray(words).view(ml_dtypes.float8_e4m3fn).astype(np.float64)
    else:
        nib = np.empty((g, p, n, 4), np.uint8)
        nib[..., 0::2] = words & 0xF
        nib[..., 1::2] = words >> 4
        vals = E2M1[nib]
    vals = vals * np.repeat(np.exp2(scales.astype(np.float64) - 127.0), 8, axis=1)[..., None]
    return vals.transpose(0, 1, 3, 2).reshape(g * 512, n)
def pack4(w):
    words, scales = pack_weight(w, "e2m1")
    return words.reshape(words.shape[0], 128, -1), scales


def unpack4(words, scales):
    return unpack_weight(words.reshape(words.shape[0], 128, -1, 2), scales, "e2m1")


D, G, N = 640, 2560, 1024


def setup_inputs():
    s = mx_kscale(G)
    seeds = np.random.standard_normal((D, G)) * s
    far = np.random.standard_normal((G, N)) / np.sqrt(G) / s[:, None]
    walk = np.random.standard_normal((G, N)) / np.sqrt(G) / s[:, None]
    modules = np.random.standard_normal((G, N)) / np.sqrt(G) / s[:, None]
    far_words, far_scales = pack4(far)
    walk_words, walk_scales = pack_weight(walk, "e4m3")
    return {"seeds": bf(seeds),
            "far_words": far_words,
            "far_scales": far_scales,
            "walk_words": walk_words,
            "walk_scales": walk_scales,
            "modules": bf(modules)}


def reference(seeds, far_words, far_scales, walk_words, walk_scales, modules):
    x = mxq(f64(seeds), 1, "e4m3")
    far = unpack4(far_words, far_scales)
    walk = unpack_weight(walk_words, walk_scales, "e4m3")
    near = mxq(f64(modules), 0, "e4m3")
    diffused = x @ far
    odds = np.exp(x @ walk)
    direct = x @ near
    return diffused + (direct - diffused) / (1.0 + odds)

@@ -1,0 +1,311 @@
+from contextlib import ExitStack
+
+import concourse.mybir as mybir
+from concourse.masks import make_identity
+
+D, K, N = 640, 2560, 1024
+FLOPS = 3 * 2 * D * K * N
+
+F32 = mybir.dt.float32
+BF16 = mybir.dt.bfloat16
+U32 = mybir.dt.uint32
+I32 = mybir.dt.int32
+U8 = mybir.dt.uint8
+E4M3 = mybir.dt.float8_e4m3fn_x4
+E2M1 = mybir.dt.float4_e2m1fn_x4
+ALU = mybir.AluOpType
+SIGMOID = mybir.ActivationFunctionType.Sigmoid
+
+P = 128
+G = K // 512
+MT = D // P
+NH = 512
+H = N // NH
+
+
+def tile_drug_restart_scores_s10_kernel(
+    tc, seeds, far_words, far_scales, walk_words, walk_scales, modules, out
+):
+    nc = tc.nc
+    with ExitStack() as ctx:
+        keep = ctx.enter_context(tc.tile_pool(name="keep", bufs=1))
+        stage = ctx.enter_context(tc.tile_pool(name="stage", bufs=2))
+        psum = ctx.enter_context(tc.psum_pool(name="psum", bufs=8))
+        ctx.enter_context(tc.manual_schedule())
+
+        ident = keep.tile([P, P], F32, name="ident", align_bytes=64)
+        warm = keep.tile([P, 2], F32, name="warm", align_bytes=64)
+        x_raw = [keep.tile([P, K], BF16, name="x_raw%d" % m, align_bytes=64) for m in range(MT)]
+        x_codes = [keep.tile([P, G, P], U32, name="x_codes%d" % m, align_bytes=64) for m in range(MT)]
+        x_scales = [keep.tile([P, G, P], U8, name="x_scales%d" % m, align_bytes=64) for m in range(MT)]
+        f_words = keep.tile([P, G, 2 * N], U8, name="f_words", align_bytes=64)
+        f_scales = keep.tile([P, G, N], U8, name="f_scales", align_bytes=64)
+        w_words = keep.tile([P, G, N], U32, name="w_words", align_bytes=64)
+        w_scales = keep.tile([P, G, N], U8, name="w_scales", align_bytes=64)
+        d_raw = [keep.tile([P, 4, N], BF16, name="d_raw%d" % g, align_bytes=64) for g in range(G)]
+        d_codes = keep.tile([P, G, N], U32, name="d_codes", align_bytes=64)
+        d_scales = keep.tile([P, G, N], U8, name="d_scales", align_bytes=64)
+        pairs = [(m, h) for h in range(H) for m in range(MT)]
+        f_sb = {mh: keep.tile([P, NH], F32, name="f_sb%d%d" % mh, align_bytes=64) for mh in pairs}
+        r_sb = {mh: keep.tile([P, NH], F32, name="r_sb%d%d" % mh, align_bytes=64) for mh in pairs}
+
+        def load_x(m, k0, k1):
+            nc.sync.dma_start(out=x_raw[m][:, k0:k1], in_=seeds[m * P : (m + 1) * P, k0:k1])
+
+        def load_far(g0, g1, h):
+            w = NH // 2
+            nc.sync.dma_start(
+                out=f_words[:].bitcast(I32)[:, g0:g1, h * w : (h + 1) * w],
+                in_=far_words.bitcast(I32)[g0:g1, :, h * w : (h + 1) * w].rearrange("g p w -> p g w"),
+            )
+
+        def load_walk(h):
+            nc.sync.dma_start(
+                out=w_words[:].bitcast(I32)[:, :, h * NH : (h + 1) * NH],
+                in_=walk_words.rearrange("g p n t -> g p (n t)").bitcast(I32)[:, :, h * NH : (h + 1) * NH].rearrange(
+                    "g p w -> p g w"
+                ),
+            )
+
+        def load_scales(tile, dram):
+            for r in range(4):
+                nc.sync.dma_start(
+                    out=tile[:].bitcast(I32)[r:P:32, :, :],
+                    in_=dram.bitcast(I32)[:, r:16:4, :].rearrange("g q w -> q g w"),
+                )
+
+        def load_modules(g):
+            nc.sync.dma_start(
+                out=d_raw[g][:], in_=modules[512 * g : 512 * (g + 1), :].rearrange("(p j) w -> p j w", j=4)
+            )
+
+        nc.vector.memset(f_scales[:].bitcast(I32), 0)
+        nc.vector.memset(warm[:], 0.0)
+        nc.vector.memset(w_scales[:].bitcast(I32), 0)
+        make_identity(nc, ident[:])
+        nc.scalar.activation(out=warm[:, 1:2], in_=warm[:, 0:1], func=SIGMOID)
+
+        load_x(0, 0, 1024)
+        load_scales(f_scales, far_scales)
+        load_far(0, 2, 0)
+        load_x(0, 1024, K)
+        load_far(2, 5, 0)
+        load_x(1, 0, K)
+        load_far(0, 5, 1)
+        load_x(2, 0, K)
+        load_x(3, 0, K)
+        load_x(4, 0, K)
+        load_modules(0)
+        load_modules(1)
+        load_scales(w_scales, walk_scales)
+        load_walk(0)
+        load_modules(2)
+        load_walk(1)
+        load_modules(3)
+        load_modules(4)
+
+        spans = [(0, 2), (2, 4), (4, 5)]
+        banks = {}
+        grouped = {}
+        ordered = {}
+
+        def reorder_x(m):
+            t = stage.tile([P, G, 2, P], F32, name="x_ordered", align_bytes=64)
+            nc.scalar.copy(out=t[:], in_=x_raw[m][:].bitcast(F32).rearrange("r (g p u) -> r g u p", u=2, p=P))
+            ordered[m] = t
+
+        def transpose_x(m, s):
+            g0, g1 = spans[s]
+            bank = psum.tile([P, 2, 2, P], F32, name="bank")
+            for g in range(g0, g1):
+                for u in range(2):
+                    if m in ordered:
+                        src = ordered[m][:, g, u, :]
+                    else:
+                        src = x_raw[m][:].bitcast(F32)[:, 256 * g + u : 256 * (g + 1) : 2]
+                    nc.tensor.transpose(bank[:, g - g0, u, :], src, ident[:])
+            banks[m, s] = bank
+
+        def copy_x(m, s, engine_copy):
+            g0, g1 = spans[s]
+            t = stage.tile([P, 2, P, 4], BF16, name="x_grouped%d" % s, align_bytes=64)
+            n = g1 - g0
+            engine_copy(
+                out=t[:].bitcast(F32)[:, 0:n, :, :], in_=banks[m, s][:, 0:n, :, :].rearrange("p g u r -> p g r u")
+            )
+            grouped[m, s] = t
+
+        def quantize_x(m, s):
+            g0, g1 = spans[s]
+            n = g1 - g0
+            nc.vector.quantize_mx(
+                out=x_codes[m][:, g0:g1, :].rearrange("p g r -> p (g r)").bitcast(E4M3),
+                scales=x_scales[m][:, g0:g1, :].rearrange("p g r -> p (g r)"),
+                in_=grouped[m, s][:, 0:n, :, :].rearrange("p g r j -> p (g r j)"),
+            )
+
+        vcopy = nc.vector.tensor_copy
+        scopy = nc.scalar.copy
+
+        d_grouped = {}
+
+        def copy_d(g, h, engine_copy):
+            t = stage.tile([P, NH, 4], BF16, name="d_grouped", align_bytes=64, bufs=3)
+            engine_copy(
+                out=t[:].rearrange("p (c i) j -> p c j i", i=4),
+                in_=d_raw[g][:, :, h * NH : (h + 1) * NH].rearrange("p j (c i) -> p c j i", i=4),
+            )
+            d_grouped[g, h] = t
+
+        def quantize_d(g, h):
+            cols = slice(h * NH, (h + 1) * NH)
+            nc.vector.quantize_mx(
+                out=d_codes[:, g, cols].bitcast(E4M3),
+                scales=d_scales[:, g, cols],
+                in_=d_grouped[g, h][:].rearrange("p w j -> p (w j)"),
+            )
+
+        acc = {}
+
+        def product(kind, m, h, c0=0, c1=NH):
+            bank = psum.tile([P, NH], F32, name="bank")
+            n0, n1 = h * NH + c0, h * NH + c1
+            for g in range(G):
+                if kind == "far":
+                    rhs, scale = f_words[:, g, 2 * n0 : 2 * n1].bitcast(E2M1), f_scales[:, g, n0:n1]
+                elif kind == "walk":
+                    rhs, scale = w_words[:, g, n0:n1].bitcast(E4M3), w_scales[:, g, n0:n1]
+                else:
+                    rhs, scale = d_codes[:, g, n0:n1].bitcast(E4M3), d_scales[:, g, n0:n1]
+                nc.tensor.matmul_mx(
+                    out=bank[:, c0:c1],
+                    lhsT=x_codes[m][:, g, :].bitcast(E4M3),
+                    lhsT_scale=x_scales[m][:, g, :],
+                    rhs=rhs,
+                    rhs_scale=scale,
+                    start=(g == 0),
+                    stop=(g == G - 1),
+                )
+            acc[kind, m, h, c0] = bank
+
+        def keep_far(m, h):
+            nc.scalar.copy(out=f_sb[m, h][:], in_=acc["far", m, h, 0][:])
+
+        def restart(m, h):
+            nc.scalar.activation(out=r_sb[m, h][:], in_=acc["walk", m, h, 0][:], func=SIGMOID, scale=-1.0)
+
+        def weigh_far(m, h):
+            nc.vector.scalar_tensor_tensor(
+                out=f_sb[m, h][:], in0=r_sb[m, h][:], scalar=1.0, in1=f_sb[m, h][:], op0=ALU.subtract, op1=ALU.mult
+            )
+
+        def weigh_direct(m, h, c0=0, c1=NH):
+            r = r_sb[m, h][:, c0:c1]
+            nc.vector.tensor_tensor(out=r, in0=acc["direct", m, h, c0][:, c0:c1], in1=r, op=ALU.mult)
+
+        def add_up(m, h, engine, c0=0, c1=NH):
+            r = r_sb[m, h][:, c0:c1]
+            engine.tensor_tensor(out=r, in0=r, in1=f_sb[m, h][:, c0:c1], op=ALU.subtract)
+            nc.sync.dma_start(out=out[m * P : (m + 1) * P, h * NH + c0 : h * NH + c1], in_=r)
+
+        transpose_x(0, 0)
+        transpose_x(0, 1)
+        transpose_x(0, 2)
+        copy_x(0, 0, vcopy)
+        copy_x(0, 1, scopy)
+        quantize_x(0, 0)
+        copy_x(0, 2, vcopy)
+        quantize_x(0, 1)
+        quantize_x(0, 2)
+
+        def bring_x(m):
+            for s in range(3):
+                transpose_x(m, s)
+
+        def take_x(m):
+            copy_x(m, 0, vcopy)
+            copy_x(m, 1, scopy)
+            copy_x(m, 2, vcopy)
+            for s in range(3):
+                quantize_x(m, s)
+
+        product("far", 0, 0)
+        bring_x(1)
+        take_x(1)
+        product("far", 0, 1)
+        keep_far(0, 0)
+        product("far", 1, 0)
+        reorder_x(2)
+        keep_far(0, 1)
+        bring_x(2)
+        take_x(2)
+        product("far", 1, 1)
+        reorder_x(3)
+        keep_far(1, 0)
+        reorder_x(4)
+        product("far", 2, 0)
+        keep_far(1, 1)
+        bring_x(3)
+        take_x(3)
+        bring_x(4)
+        take_x(4)
+        product("far", 2, 1)
+        keep_far(2, 0)
+        copy_d(0, 0, vcopy)
+        product("far", 3, 0)
+        keep_far(2, 1)
+        copy_d(0, 1, vcopy)
+        quantize_d(0, 0)
+        product("far", 3, 1)
+        keep_far(3, 0)
+        copy_d(1, 0, vcopy)
+        quantize_d(0, 1)
+        product("far", 4, 0)
+        keep_far(3, 1)
+        copy_d(1, 1, vcopy)
+        quantize_d(1, 0)
+        product("far", 4, 1)
+        keep_far(4, 0)
+        quantize_d(1, 1)
+
+        scalar_chunks = {0: (2, 0), 2: (2, 1), 5: (3, 1), 7: (4, 1)}
+        vector_chunks = {4: (3, 0), 6: (4, 0)}
+        quantize_at = {3: (2, 0), 5: (3, 0), 6: (2, 1), 7: (4, 0), 9: (3, 1)}
+        for i, (m, h) in enumerate(pairs):
+            product("walk", m, h)
+            if i == 0:
+                keep_far(4, 1)
+            else:
+                restart(*pairs[i - 1])
+            if i in scalar_chunks:
+                copy_d(*scalar_chunks[i], scopy)
+            if i in vector_chunks:
+                copy_d(*vector_chunks[i], vcopy)
+            if i >= 2:
+                weigh_far(*pairs[i - 2])
+            if i in quantize_at:
+                quantize_d(*quantize_at[i])
+
+        last = len(pairs) - 1
+        for i, (m, h) in enumerate(pairs):
+            if i < last:
+                product("direct", m, h)
+            else:
+                product("direct", m, h, 0, 256)
+                product("direct", m, h, 256, 512)
+            if i == 0:
+                restart(*pairs[last])
+                weigh_far(*pairs[last - 1])
+                quantize_d(4, 1)
+            elif i == 1:
+                weigh_far(*pairs[last])
+                weigh_direct(*pairs[0])
+                add_up(*pairs[0], nc.gpsimd)
+            else:
+                weigh_direct(*pairs[i - 1])
+                add_up(*pairs[i - 1], nc.gpsimd if i < last else nc.vector)
+        m, h = pairs[last]
+        weigh_direct(m, h, 0, 256)
+        add_up(m, h, nc.vector, 0, 256)
+        weigh_direct(m, h, 256, 512)
+        add_up(m, h, nc.vector, 256, 512)

@@ -33,21 +33,21 @@ def tile_drug_restart_scores_s10_kernel(
         psum = ctx.enter_context(tc.psum_pool(name="psum", bufs=8))
         ctx.enter_context(tc.manual_schedule())
 
-        ident = keep.tile([P, P], F32, name="ident", align_bytes=64)
-        warm = keep.tile([P, 2], F32, name="warm", align_bytes=64)
-        x_raw = [keep.tile([P, K], BF16, name="x_raw%d" % m, align_bytes=64) for m in range(MT)]
-        x_codes = [keep.tile([P, G, P], U32, name="x_codes%d" % m, align_bytes=64) for m in range(MT)]
-        x_scales = [keep.tile([P, G, P], U8, name="x_scales%d" % m, align_bytes=64) for m in range(MT)]
-        f_words = keep.tile([P, G, 2 * N], U8, name="f_words", align_bytes=64)
-        f_scales = keep.tile([P, G, N], U8, name="f_scales", align_bytes=64)
-        w_words = keep.tile([P, G, N], U32, name="w_words", align_bytes=64)
-        w_scales = keep.tile([P, G, N], U8, name="w_scales", align_bytes=64)
-        d_raw = [keep.tile([P, 4, N], BF16, name="d_raw%d" % g, align_bytes=64) for g in range(G)]
-        d_codes = keep.tile([P, G, N], U32, name="d_codes", align_bytes=64)
-        d_scales = keep.tile([P, G, N], U8, name="d_scales", align_bytes=64)
+        ident = keep.tile([P, P], F32, name="ident", align_bytes=256)
+        warm = keep.tile([P, 2], F32, name="warm", align_bytes=256)
+        x_raw = [keep.tile([P, K], BF16, name="x_raw%d" % m, align_bytes=256) for m in range(MT)]
+        x_codes = [keep.tile([P, G, P], U32, name="x_codes%d" % m, align_bytes=256) for m in range(MT)]
+        x_scales = [keep.tile([P, G, P], U8, name="x_scales%d" % m, align_bytes=256) for m in range(MT)]
+        f_words = keep.tile([P, G, 2 * N], U8, name="f_words", align_bytes=256)
+        f_scales = keep.tile([P, G, N], U8, name="f_scales", align_bytes=256)
+        w_words = keep.tile([P, G, N], U32, name="w_words", align_bytes=256)
+        w_scales = keep.tile([P, G, N], U8, name="w_scales", align_bytes=256)
+        d_raw = [[keep.tile([P, 4, NH], BF16, name="d_raw%d%d" % (g, h), align_bytes=256) for h in range(H)] for g in range(G)]
+        d_codes = keep.tile([P, G, N], U32, name="d_codes", align_bytes=256)
+        d_scales = keep.tile([P, G, N], U8, name="d_scales", align_bytes=256)
         pairs = [(m, h) for h in range(H) for m in range(MT)]
-        f_sb = {mh: keep.tile([P, NH], F32, name="f_sb%d%d" % mh, align_bytes=64) for mh in pairs}
-        r_sb = {mh: keep.tile([P, NH], F32, name="r_sb%d%d" % mh, align_bytes=64) for mh in pairs}
+        f_sb = {mh: keep.tile([P, NH], F32, name="f_sb%d%d" % mh, align_bytes=256) for mh in pairs}
+        r_sb = {mh: keep.tile([P, NH], F32, name="r_sb%d%d" % mh, align_bytes=256) for mh in pairs}
 
         def load_x(m, k0, k1):
             nc.sync.dma_start(out=x_raw[m][:, k0:k1], in_=seeds[m * P : (m + 1) * P, k0:k1])
@@ -59,12 +59,11 @@ def tile_drug_restart_scores_s10_kernel(
                 in_=far_words.bitcast(I32)[g0:g1, :, h * w : (h + 1) * w].rearrange("g p w -> p g w"),
             )
 
-        def load_walk(h):
+        def load_walk(g0, g1, h):
+            words = walk_words.rearrange("g p n t -> g p (n t)").bitcast(I32)
             nc.sync.dma_start(
-                out=w_words[:].bitcast(I32)[:, :, h * NH : (h + 1) * NH],
-                in_=walk_words.rearrange("g p n t -> g p (n t)").bitcast(I32)[:, :, h * NH : (h + 1) * NH].rearrange(
-                    "g p w -> p g w"
-                ),
+                out=w_words[:].bitcast(I32)[:, g0:g1, h * NH : (h + 1) * NH],
+                in_=words[g0:g1, :, h * NH : (h + 1) * NH].rearrange("g p w -> p g w"),
             )
 
         def load_scales(tile, dram):
@@ -74,12 +73,29 @@ def tile_drug_restart_scores_s10_kernel(
                     in_=dram.bitcast(I32)[:, r:16:4, :].rearrange("g q w -> q g w"),
                 )
 
-        def load_modules(g):
-            nc.sync.dma_start(
-                out=d_raw[g][:], in_=modules[512 * g : 512 * (g + 1), :].rearrange("(p j) w -> p j w", j=4)
-            )
+        def load_modules(g, h):
+            rows = modules[512 * g : 512 * (g + 1), h * NH : (h + 1) * NH]
+            nc.sync.dma_start(out=d_raw[g][h][:], in_=rows.rearrange("(p j) w -> p j w", j=4))
 
-        nc.vector.memset(f_scales[:].bitcast(I32), 0)
+        nc.gpsimd.memset(f_scales[:].bitcast(I32)[:, :, 0:128], 0)
+        nc.vector.memset(f_scales[:].bitcast(I32)[:, :, 128:256], 0)
+        nc.gpsimd.memset(d_codes[:, G - 1, 0:NH], 0)
+        nc.gpsimd.memset(d_scales[:, G - 1, 0:NH].bitcast(I32), 0)
+
+        def busy(count):
+            bank = psum.tile([P, NH], F32, name="bank")
+            for i in range(count):
+                nc.tensor.matmul_mx(
+                    out=bank[:],
+                    lhsT=d_codes[:, G - 1, 0:P].bitcast(E4M3),
+                    lhsT_scale=d_scales[:, G - 1, 0:P],
+                    rhs=d_codes[:, G - 1, 0:NH].bitcast(E4M3),
+                    rhs_scale=d_scales[:, G - 1, 0:NH],
+                    start=True,
+                    stop=True,
+                )
+
+
         nc.vector.memset(warm[:], 0.0)
         nc.vector.memset(w_scales[:].bitcast(I32), 0)
         make_identity(nc, ident[:])
@@ -93,25 +109,30 @@ def tile_drug_restart_scores_s10_kernel(
         load_x(1, 0, K)
         load_far(0, 5, 1)
         load_x(2, 0, K)
+        load_modules(0, 0)
         load_x(3, 0, K)
         load_x(4, 0, K)
-        load_modules(0)
-        load_modules(1)
         load_scales(w_scales, walk_scales)
-        load_walk(0)
-        load_modules(2)
-        load_walk(1)
-        load_modules(3)
-        load_modules(4)
+        load_modules(1, 0)
+        load_walk(0, 5, 0)
+        load_modules(2, 0)
+        load_modules(3, 0)
+        load_modules(4, 0)
+        load_modules(0, 1)
+        load_modules(1, 1)
+        load_walk(0, 5, 1)
+        load_modules(2, 1)
+        load_modules(3, 1)
+        load_modules(4, 1)
 
         spans = [(0, 2), (2, 4), (4, 5)]
         banks = {}
         grouped = {}
         ordered = {}
 
-        def reorder_x(m):
-            t = stage.tile([P, G, 2, P], F32, name="x_ordered", align_bytes=64)
-            nc.scalar.copy(out=t[:], in_=x_raw[m][:].bitcast(F32).rearrange("r (g p u) -> r g u p", u=2, p=P))
+        def reorder_x(m, engine_copy):
+            t = stage.tile([P, G, 2, P], F32, name="x_ordered", align_bytes=256)
+            engine_copy(out=t[:], in_=x_raw[m][:].bitcast(F32).rearrange("r (g p u) -> r g u p", u=2, p=P))
             ordered[m] = t
 
         def transpose_x(m, s):
@@ -128,7 +149,7 @@ def tile_drug_restart_scores_s10_kernel(
 
         def copy_x(m, s, engine_copy):
             g0, g1 = spans[s]
-            t = stage.tile([P, 2, P, 4], BF16, name="x_grouped%d" % s, align_bytes=64)
+            t = stage.tile([P, 2, P, 4], BF16, name="x_grouped%d" % s, align_bytes=256)
             n = g1 - g0
             engine_copy(
                 out=t[:].bitcast(F32)[:, 0:n, :, :], in_=banks[m, s][:, 0:n, :, :].rearrange("p g u r -> p g r u")
@@ -149,13 +170,13 @@ def tile_drug_restart_scores_s10_kernel(
 
         d_grouped = {}
 
-        def copy_d(g, h, engine_copy):
-            t = stage.tile([P, NH, 4], BF16, name="d_grouped", align_bytes=64, bufs=3)
+        def copy_d(g, h, engine_copy, c0=0, c1=NH):
+            if c0 == 0:
+                d_grouped[g, h] = stage.tile([P, NH, 4], BF16, name="d_grouped", align_bytes=256, bufs=4)
             engine_copy(
-                out=t[:].rearrange("p (c i) j -> p c j i", i=4),
-                in_=d_raw[g][:, :, h * NH : (h + 1) * NH].rearrange("p j (c i) -> p c j i", i=4),
+                out=d_grouped[g, h][:, c0:c1, :].rearrange("p (c i) j -> p c j i", i=4),
+                in_=d_raw[g][h][:, :, c0:c1].rearrange("p j (c i) -> p c j i", i=4),
             )
-            d_grouped[g, h] = t
 
         def quantize_d(g, h):
             cols = slice(h * NH, (h + 1) * NH)
@@ -203,12 +224,13 @@ def tile_drug_restart_scores_s10_kernel(
             r = r_sb[m, h][:, c0:c1]
             nc.vector.tensor_tensor(out=r, in0=acc["direct", m, h, c0][:, c0:c1], in1=r, op=ALU.mult)
 
-        def add_up(m, h, engine, c0=0, c1=NH):
+        def add_up(m, h, c0=0, c1=NH):
             r = r_sb[m, h][:, c0:c1]
-            engine.tensor_tensor(out=r, in0=r, in1=f_sb[m, h][:, c0:c1], op=ALU.subtract)
+            nc.vector.tensor_tensor(out=r, in0=r, in1=f_sb[m, h][:, c0:c1], op=ALU.subtract)
             nc.sync.dma_start(out=out[m * P : (m + 1) * P, h * NH + c0 : h * NH + c1], in_=r)
 
         transpose_x(0, 0)
+        busy(2)
         transpose_x(0, 1)
         transpose_x(0, 2)
         copy_x(0, 0, vcopy)
@@ -230,19 +252,21 @@ def tile_drug_restart_scores_s10_kernel(
                 quantize_x(m, s)
 
         product("far", 0, 0)
+        reorder_x(1, vcopy)
         bring_x(1)
         take_x(1)
         product("far", 0, 1)
         keep_far(0, 0)
         product("far", 1, 0)
-        reorder_x(2)
+        reorder_x(2, scopy)
         keep_far(0, 1)
         bring_x(2)
         take_x(2)
         product("far", 1, 1)
-        reorder_x(3)
+        reorder_x(3, scopy)
+        reorder_x(4, vcopy)
+        copy_d(0, 0, vcopy)
         keep_far(1, 0)
-        reorder_x(4)
         product("far", 2, 0)
         keep_far(1, 1)
         bring_x(3)
@@ -251,61 +275,55 @@ def tile_drug_restart_scores_s10_kernel(
         take_x(4)
         product("far", 2, 1)
         keep_far(2, 0)
-        copy_d(0, 0, vcopy)
+        quantize_d(0, 0)
         product("far", 3, 0)
         keep_far(2, 1)
-        copy_d(0, 1, vcopy)
-        quantize_d(0, 0)
+        copy_d(1, 0, scopy)
+        copy_d(2, 0, vcopy)
         product("far", 3, 1)
         keep_far(3, 0)
-        copy_d(1, 0, vcopy)
-        quantize_d(0, 1)
+        quantize_d(1, 0)
+        quantize_d(2, 0)
         product("far", 4, 0)
         keep_far(3, 1)
-        copy_d(1, 1, vcopy)
-        quantize_d(1, 0)
+        copy_d(3, 0, scopy)
         product("far", 4, 1)
         keep_far(4, 0)
-        quantize_d(1, 1)
+        copy_d(4, 0, vcopy)
 
-        scalar_chunks = {0: (2, 0), 2: (2, 1), 5: (3, 1), 7: (4, 1)}
-        vector_chunks = {4: (3, 0), 6: (4, 0)}
-        quantize_at = {3: (2, 0), 5: (3, 0), 6: (2, 1), 7: (4, 0), 9: (3, 1)}
-        for i, (m, h) in enumerate(pairs):
-            product("walk", m, h)
-            if i == 0:
+        steps = [(kind, m, h) for h in range(H) for kind in ("walk", "direct") for m in range(MT)]
+        last = len(steps) - 1
+        scalar_parts = {3: (1, 0), 4: (1, 1), 6: (2, 0), 7: (2, 1), 8: (3, 0), 9: (3, 1), 10: (4, 0), 11: (4, 1)}
+        vector_chunks = {1: (0, 1)}
+        quantize_at = {0: [(3, 0)], 1: [(4, 0)], 2: [(0, 1)], 6: [(1, 1)], 9: [(2, 1)], 11: [(3, 1)], 13: [(4, 1)]}
+        for s, (kind, m, h) in enumerate(steps):
+            if s < last:
+                product(kind, m, h)
+            else:
+                product(kind, m, h, 0, 256)
+                product(kind, m, h, 256, 512)
+            if s == 0:
                 keep_far(4, 1)
-            else:
-                restart(*pairs[i - 1])
-            if i in scalar_chunks:
-                copy_d(*scalar_chunks[i], scopy)
-            if i in vector_chunks:
-                copy_d(*vector_chunks[i], vcopy)
-            if i >= 2:
-                weigh_far(*pairs[i - 2])
-            if i in quantize_at:
-                quantize_d(*quantize_at[i])
-
-        last = len(pairs) - 1
-        for i, (m, h) in enumerate(pairs):
-            if i < last:
-                product("direct", m, h)
-            else:
-                product("direct", m, h, 0, 256)
-                product("direct", m, h, 256, 512)
-            if i == 0:
-                restart(*pairs[last])
-                weigh_far(*pairs[last - 1])
-                quantize_d(4, 1)
-            elif i == 1:
-                weigh_far(*pairs[last])
-                weigh_direct(*pairs[0])
-                add_up(*pairs[0], nc.gpsimd)
-            else:
-                weigh_direct(*pairs[i - 1])
-                add_up(*pairs[i - 1], nc.gpsimd if i < last else nc.vector)
-        m, h = pairs[last]
+            elif steps[s - 1][0] == "walk":
+                restart(*steps[s - 1][1:])
+            if s in vector_chunks:
+                copy_d(*vector_chunks[s], vcopy)
+            if s in scalar_parts:
+                g, part = scalar_parts[s]
+                copy_d(g, 1, scopy, 256 * part, 256 * (part + 1))
+            for chunk in quantize_at.get(s, []):
+                quantize_d(*chunk)
+            if s >= 2:
+                before, mb, hb = steps[s - 2]
+                if before == "walk":
+                    weigh_far(mb, hb)
+                else:
+                    add_up(mb, hb)
+            if s >= 1 and steps[s - 1][0] == "direct":
+                weigh_direct(*steps[s - 1][1:])
+        m, h = steps[last][1:]
         weigh_direct(m, h, 0, 256)
-        add_up(m, h, nc.vector, 0, 256)
+        add_up(m - 1, h)
         weigh_direct(m, h, 256, 512)
-        add_up(m, h, nc.vector, 256, 512)
+        add_up(m, h, 0, 256)
+        add_up(m, h, 256, 512)

from contextlib import ExitStack

import concourse.mybir as mybir
from concourse.masks import make_identity

D, K, N = 640, 2560, 1024
FLOPS = 3 * 2 * D * K * N

F32 = mybir.dt.float32
BF16 = mybir.dt.bfloat16
U32 = mybir.dt.uint32
I32 = mybir.dt.int32
U8 = mybir.dt.uint8
E4M3 = mybir.dt.float8_e4m3fn_x4
E2M1 = mybir.dt.float4_e2m1fn_x4
ALU = mybir.AluOpType
SIGMOID = mybir.ActivationFunctionType.Sigmoid

P = 128
G = K // 512
MT = D // P
NH = 512
H = N // NH


def tile_drug_restart_scores_s10_kernel(
    tc, seeds, far_words, far_scales, walk_words, walk_scales, modules, out
):
    nc = tc.nc
    with ExitStack() as ctx:
        keep = ctx.enter_context(tc.tile_pool(name="keep", bufs=1))
        stage = ctx.enter_context(tc.tile_pool(name="stage", bufs=2))
        psum = ctx.enter_context(tc.psum_pool(name="psum", bufs=8))
        ctx.enter_context(tc.manual_schedule())

        ident = keep.tile([P, P], F32, name="ident", align_bytes=256)
        warm = keep.tile([P, 2], F32, name="warm", align_bytes=256)
        x_raw = [keep.tile([P, K], BF16, name="x_raw%d" % m, align_bytes=256) for m in range(MT)]
        x_codes = [keep.tile([P, G, P], U32, name="x_codes%d" % m, align_bytes=256) for m in range(MT)]
        x_scales = [keep.tile([P, G, P], U8, name="x_scales%d" % m, align_bytes=256) for m in range(MT)]
        f_words = keep.tile([P, G, 2 * N], U8, name="f_words", align_bytes=256)
        f_scales = keep.tile([P, G, N], U8, name="f_scales", align_bytes=256)
        w_words = keep.tile([P, G, N], U32, name="w_words", align_bytes=256)
        w_scales = keep.tile([P, G, N], U8, name="w_scales", align_bytes=256)
        d_raw = [[keep.tile([P, 4, NH], BF16, name="d_raw%d%d" % (g, h), align_bytes=256) for h in range(H)] for g in range(G)]
        d_codes = keep.tile([P, G, N], U32, name="d_codes", align_bytes=256)
        d_scales = keep.tile([P, G, N], U8, name="d_scales", align_bytes=256)
        pairs = [(m, h) for h in range(H) for m in range(MT)]
        f_sb = {mh: keep.tile([P, NH], F32, name="f_sb%d%d" % mh, align_bytes=256) for mh in pairs}
        r_sb = {mh: keep.tile([P, NH], F32, name="r_sb%d%d" % mh, align_bytes=256) for mh in pairs}

        def load_x(m, k0, k1):
            nc.sync.dma_start(out=x_raw[m][:, k0:k1], in_=seeds[m * P : (m + 1) * P, k0:k1])

        def load_far(g0, g1, h):
            w = NH // 2
            nc.sync.dma_start(
                out=f_words[:].bitcast(I32)[:, g0:g1, h * w : (h + 1) * w],
                in_=far_words.bitcast(I32)[g0:g1, :, h * w : (h + 1) * w].rearrange("g p w -> p g w"),
            )

        def load_walk(g0, g1, h):
            words = walk_words.rearrange("g p n t -> g p (n t)").bitcast(I32)
            nc.sync.dma_start(
                out=w_words[:].bitcast(I32)[:, g0:g1, h * NH : (h + 1) * NH],
                in_=words[g0:g1, :, h * NH : (h + 1) * NH].rearrange("g p w -> p g w"),
            )

        def load_scales(tile, dram):
            for r in range(4):
                nc.sync.dma_start(
                    out=tile[:].bitcast(I32)[r:P:32, :, :],
                    in_=dram.bitcast(I32)[:, r:16:4, :].rearrange("g q w -> q g w"),
                )

        def load_modules(g, h):
            rows = modules[512 * g : 512 * (g + 1), h * NH : (h + 1) * NH]
            nc.sync.dma_start(out=d_raw[g][h][:], in_=rows.rearrange("(p j) w -> p j w", j=4))

        nc.gpsimd.memset(f_scales[:].bitcast(I32)[:, :, 0:128], 0)
        nc.vector.memset(f_scales[:].bitcast(I32)[:, :, 128:256], 0)
        nc.gpsimd.memset(d_codes[:, G - 1, 0:NH], 0)
        nc.gpsimd.memset(d_scales[:, G - 1, 0:NH].bitcast(I32), 0)

        def busy(count):
            bank = psum.tile([P, NH], F32, name="bank")
            for i in range(count):
                nc.tensor.matmul_mx(
                    out=bank[:],
                    lhsT=d_codes[:, G - 1, 0:P].bitcast(E4M3),
                    lhsT_scale=d_scales[:, G - 1, 0:P],
                    rhs=d_codes[:, G - 1, 0:NH].bitcast(E4M3),
                    rhs_scale=d_scales[:, G - 1, 0:NH],
                    start=True,
                    stop=True,
                )


        nc.vector.memset(warm[:], 0.0)
        nc.vector.memset(w_scales[:].bitcast(I32), 0)
        make_identity(nc, ident[:])
        nc.scalar.activation(out=warm[:, 1:2], in_=warm[:, 0:1], func=SIGMOID)

        load_x(0, 0, 1024)
        load_scales(f_scales, far_scales)
        load_far(0, 2, 0)
        load_x(0, 1024, K)
        load_far(2, 5, 0)
        load_x(1, 0, K)
        load_far(0, 5, 1)
        load_x(2, 0, K)
        load_modules(0, 0)
        load_x(3, 0, K)
        load_x(4, 0, K)
        load_scales(w_scales, walk_scales)
        load_modules(1, 0)
        load_walk(0, 5, 0)
        load_modules(2, 0)
        load_modules(3, 0)
        load_modules(4, 0)
        load_modules(0, 1)
        load_modules(1, 1)
        load_walk(0, 5, 1)
        load_modules(2, 1)
        load_modules(3, 1)
        load_modules(4, 1)

        spans = [(0, 2), (2, 4), (4, 5)]
        banks = {}
        grouped = {}
        ordered = {}

        def reorder_x(m, engine_copy):
            t = stage.tile([P, G, 2, P], F32, name="x_ordered", align_bytes=256)
            engine_copy(out=t[:], in_=x_raw[m][:].bitcast(F32).rearrange("r (g p u) -> r g u p", u=2, p=P))
            ordered[m] = t

        def transpose_x(m, s):
            g0, g1 = spans[s]
            bank = psum.tile([P, 2, 2, P], F32, name="bank")
            for g in range(g0, g1):
                for u in range(2):
                    if m in ordered:
                        src = ordered[m][:, g, u, :]
                    else:
                        src = x_raw[m][:].bitcast(F32)[:, 256 * g + u : 256 * (g + 1) : 2]
                    nc.tensor.transpose(bank[:, g - g0, u, :], src, ident[:])
            banks[m, s] = bank

        def copy_x(m, s, engine_copy):
            g0, g1 = spans[s]
            t = stage.tile([P, 2, P, 4], BF16, name="x_grouped%d" % s, align_bytes=256)
            n = g1 - g0
            engine_copy(
                out=t[:].bitcast(F32)[:, 0:n, :, :], in_=banks[m, s][:, 0:n, :, :].rearrange("p g u r -> p g r u")
            )
            grouped[m, s] = t

        def quantize_x(m, s):
            g0, g1 = spans[s]
            n = g1 - g0
            nc.vector.quantize_mx(
                out=x_codes[m][:, g0:g1, :].rearrange("p g r -> p (g r)").bitcast(E4M3),
                scales=x_scales[m][:, g0:g1, :].rearrange("p g r -> p (g r)"),
                in_=grouped[m, s][:, 0:n, :, :].rearrange("p g r j -> p (g r j)"),
            )

        vcopy = nc.vector.tensor_copy
        scopy = nc.scalar.copy

        d_grouped = {}

        def copy_d(g, h, engine_copy, c0=0, c1=NH):
            if c0 == 0:
                d_grouped[g, h] = stage.tile([P, NH, 4], BF16, name="d_grouped", align_bytes=256, bufs=4)
            engine_copy(
                out=d_grouped[g, h][:, c0:c1, :].rearrange("p (c i) j -> p c j i", i=4),
                in_=d_raw[g][h][:, :, c0:c1].rearrange("p j (c i) -> p c j i", i=4),
            )

        def quantize_d(g, h):
            cols = slice(h * NH, (h + 1) * NH)
            nc.vector.quantize_mx(
                out=d_codes[:, g, cols].bitcast(E4M3),
                scales=d_scales[:, g, cols],
                in_=d_grouped[g, h][:].rearrange("p w j -> p (w j)"),
            )

        acc = {}

        def product(kind, m, h, c0=0, c1=NH):
            bank = psum.tile([P, NH], F32, name="bank")
            n0, n1 = h * NH + c0, h * NH + c1
            for g in range(G):
                if kind == "far":
                    rhs, scale = f_words[:, g, 2 * n0 : 2 * n1].bitcast(E2M1), f_scales[:, g, n0:n1]
                elif kind == "walk":
                    rhs, scale = w_words[:, g, n0:n1].bitcast(E4M3), w_scales[:, g, n0:n1]
                else:
                    rhs, scale = d_codes[:, g, n0:n1].bitcast(E4M3), d_scales[:, g, n0:n1]
                nc.tensor.matmul_mx(
                    out=bank[:, c0:c1],
                    lhsT=x_codes[m][:, g, :].bitcast(E4M3),
                    lhsT_scale=x_scales[m][:, g, :],
                    rhs=rhs,
                    rhs_scale=scale,
                    start=(g == 0),
                    stop=(g == G - 1),
                )
            acc[kind, m, h, c0] = bank

        def keep_far(m, h):
            nc.scalar.copy(out=f_sb[m, h][:], in_=acc["far", m, h, 0][:])

        def restart(m, h):
            nc.scalar.activation(out=r_sb[m, h][:], in_=acc["walk", m, h, 0][:], func=SIGMOID, scale=-1.0)

        def weigh_far(m, h):
            nc.vector.scalar_tensor_tensor(
                out=f_sb[m, h][:], in0=r_sb[m, h][:], scalar=1.0, in1=f_sb[m, h][:], op0=ALU.subtract, op1=ALU.mult
            )

        def weigh_direct(m, h, c0=0, c1=NH):
            r = r_sb[m, h][:, c0:c1]
            nc.vector.tensor_tensor(out=r, in0=acc["direct", m, h, c0][:, c0:c1], in1=r, op=ALU.mult)

        def add_up(m, h, c0=0, c1=NH):
            r = r_sb[m, h][:, c0:c1]
            nc.vector.tensor_tensor(out=r, in0=r, in1=f_sb[m, h][:, c0:c1], op=ALU.subtract)
            nc.sync.dma_start(out=out[m * P : (m + 1) * P, h * NH + c0 : h * NH + c1], in_=r)

        transpose_x(0, 0)
        busy(2)
        transpose_x(0, 1)
        transpose_x(0, 2)
        copy_x(0, 0, vcopy)
        copy_x(0, 1, scopy)
        quantize_x(0, 0)
        copy_x(0, 2, vcopy)
        quantize_x(0, 1)
        quantize_x(0, 2)

        def bring_x(m):
            for s in range(3):
                transpose_x(m, s)

        def take_x(m):
            copy_x(m, 0, vcopy)
            copy_x(m, 1, scopy)
            copy_x(m, 2, vcopy)
            for s in range(3):
                quantize_x(m, s)

        product("far", 0, 0)
        reorder_x(1, vcopy)
        bring_x(1)
        take_x(1)
        product("far", 0, 1)
        keep_far(0, 0)
        product("far", 1, 0)
        reorder_x(2, scopy)
        keep_far(0, 1)
        bring_x(2)
        take_x(2)
        product("far", 1, 1)
        reorder_x(3, scopy)
        reorder_x(4, vcopy)
        copy_d(0, 0, vcopy)
        keep_far(1, 0)
        product("far", 2, 0)
        keep_far(1, 1)
        bring_x(3)
        take_x(3)
        bring_x(4)
        take_x(4)
        product("far", 2, 1)
        keep_far(2, 0)
        quantize_d(0, 0)
        product("far", 3, 0)
        keep_far(2, 1)
        copy_d(1, 0, scopy)
        copy_d(2, 0, vcopy)
        product("far", 3, 1)
        keep_far(3, 0)
        quantize_d(1, 0)
        quantize_d(2, 0)
        product("far", 4, 0)
        keep_far(3, 1)
        copy_d(3, 0, scopy)
        product("far", 4, 1)
        keep_far(4, 0)
        copy_d(4, 0, vcopy)

        steps = [(kind, m, h) for h in range(H) for kind in ("walk", "direct") for m in range(MT)]
        last = len(steps) - 1
        scalar_parts = {3: (1, 0), 4: (1, 1), 6: (2, 0), 7: (2, 1), 8: (3, 0), 9: (3, 1), 10: (4, 0), 11: (4, 1)}
        vector_chunks = {1: (0, 1)}
        quantize_at = {0: [(3, 0)], 1: [(4, 0)], 2: [(0, 1)], 6: [(1, 1)], 9: [(2, 1)], 11: [(3, 1)], 13: [(4, 1)]}
        for s, (kind, m, h) in enumerate(steps):
            if s < last:
                product(kind, m, h)
            else:
                product(kind, m, h, 0, 256)
                product(kind, m, h, 256, 512)
            if s == 0:
                keep_far(4, 1)
            elif steps[s - 1][0] == "walk":
                restart(*steps[s - 1][1:])
            if s in vector_chunks:
                copy_d(*vector_chunks[s], vcopy)
            if s in scalar_parts:
                g, part = scalar_parts[s]
                copy_d(g, 1, scopy, 256 * part, 256 * (part + 1))
            for chunk in quantize_at.get(s, []):
                quantize_d(*chunk)
            if s >= 2:
                before, mb, hb = steps[s - 2]
                if before == "walk":
                    weigh_far(mb, hb)
                else:
                    add_up(mb, hb)
            if s >= 1 and steps[s - 1][0] == "direct":
                weigh_direct(*steps[s - 1][1:])
        m, h = steps[last][1:]
        weigh_direct(m, h, 0, 256)
        add_up(m - 1, h)
        weigh_direct(m, h, 256, 512)
        add_up(m, h, 0, 256)
        add_up(m, h, 256, 512)
